import numpy as np
import ml_dtypes


def mxq(x, axis, fmt="e4m3"):
    dtype, down = {"e4m3": (ml_dtypes.float8_e4m3fn, 7), "e5m2": (ml_dtypes.float8_e5m2, 14)}[fmt]
    v = np.moveaxis(np.asarray(x, np.float32).astype(ml_dtypes.bfloat16).astype(np.float64), axis, -1)
    blocks = v.reshape(v.shape[:-1] + (-1, 32))
    amax = np.abs(blocks).max(-1, keepdims=True)
    byte = np.maximum(np.where(amax > 0, np.frexp(amax)[1] - 1 + 127, 0) - down, 1)
    scale = np.exp2(byte - 127.0)
    codes = (blocks / scale).astype(np.float32).astype(dtype).astype(np.float64)
    return np.moveaxis((codes * scale).reshape(v.shape), -1, axis)


WIDE = False


def mx_kscale(k):
    if not WIDE:
        return np.ones(k)
    levels = np.array([10, -10, 5, -5, 0])
    if k % 512:
        return np.exp2(np.random.permutation(np.resize(levels, k // 32))).repeat(32)
    a = np.empty((k // 512, 16))
    for p in range(k // 512):
        a[p, :8] = np.random.permutation(np.resize(levels, 8))
        for g in range(8):
            far = levels[np.abs(levels - a[p, g]) >= 10]
            a[p, g + 8] = far[np.random.randint(len(far))]
    return np.exp2(a.ravel()).repeat(32)


def f64(x):
    return np.asarray(x).astype(np.float64)


E2M1 = np.array([0.0, 0.5, 1.0, 1.5, 2.0, 3.0, 4.0, 6.0, -0.0, -0.5, -1.0, -1.5, -2.0, -3.0, -4.0, -6.0])


def pack_weight(w, fmt):
    k, n = w.shape
    w = f64(np.asarray(w, np.float32).astype(ml_dtypes.bfloat16)).reshape(k // 32, 32, n)
    amax = np.abs(w).max(1)
    if fmt == "e4m3":
        byte = np.frexp(amax)[1] - 1 + 127 - 7
    else:
        mant, ex = np.frexp(amax / 6.0)
        byte = np.where(mant > 0.5, ex, ex - 1) + 127
    byte = np.clip(np.where(amax > 0, byte, 1), 1, 254)
    scaled = (w * np.exp2(127.0 - byte)[:, None, :]).reshape(k, n).astype(np.float32)
    by_word = np.ascontiguousarray(scaled.reshape(k // 512, 128, 4, n).transpose(0, 1, 3, 2))
    if fmt == "e4m3":
        words = by_word.astype(ml_dtypes.float8_e4m3fn).view(np.uint8)
    else:
        c = by_word.astype(ml_dtypes.float4_e2m1fn).view(np.uint8) & 0xF
        words = (c[..., 0::2] | (c[..., 1::2] << 4)).reshape(k // 512, 128, 2 * n)
    return np.ascontiguousarray(words), np.ascontiguousarray(byte.astype(np.uint8).reshape(k // 512, 16, n))


def unpack_weight(words, scales, fmt):
    g, _, n = scales.shape
    words = np.ascontiguousarray(words).reshape(g, 128, n, -1)
    if fmt == "e4m3":
        vals = words.view(ml_dtypes.float8_e4m3fn).astype(np.float64)
    else:
        nib = np.empty((g, 128, n, 4), np.uint8)
        nib[..., 0::2] = words & 0xF
        nib[..., 1::2] = words >> 4
        vals = E2M1[nib]
    vals = vals * np.repeat(np.exp2(scales.astype(np.float64) - 127.0), 8, axis=1)[..., None]
    return vals.transpose(0, 1, 3, 2).reshape(g * 512, n)


O, K, M, T = 512, 1024, 1024, 1024


def setup_inputs():
    n = np.random.standard_normal
    s = mx_kscale(K)[:, None]
    x = n((K, T)); x[:O] *= 6.0
    w = n((K, M)) / np.sqrt(K) / s; w[:O] /= 2.0
    p_w8 = pack_weight(w[:O], "e4m3")
    p_w4 = pack_weight(w[O:], "e2m1")
    return {
        "x": (x * s).astype(np.float32),
        "w8_words": p_w8[0],
        "w8_scales": p_w8[1],
        "w4_words": p_w4[0],
        "w4_scales": p_w4[1],
        "r": (n((1024, 1024))).astype(np.float32),
    }


def reference(x, w8_words, w8_scales, w4_words, w4_scales, r):
    x_ = mxq(f64(x), 0, "e4m3")
    w8_ = unpack_weight(w8_words, w8_scales, "e4m3")
    w4_ = unpack_weight(w4_words, w4_scales, "e2m1")
    y = x_[:O].T @ w8_ + x_[O:].T @ w4_
    return f64(r) + y

@@ -1,0 +1,119 @@
+from contextlib import ExitStack
+
+import concourse.mybir as mybir
+
+K, T, N = 1024, 1024, 1024
+FLOPS = 2 * K * T * N
+
+F32 = mybir.dt.float32
+BF16 = mybir.dt.bfloat16
+I32 = mybir.dt.int32
+U32 = mybir.dt.uint32
+U8 = mybir.dt.uint8
+FP8X4 = mybir.dt.float8_e4m3fn_x4
+FP4X4 = mybir.dt.float4_e2m1fn_x4
+
+P = 128
+PACK = 4
+K_PASS = P * PACK
+PASSES = K // K_PASS
+N_TILE = 512
+T_CHUNK = 256
+CHUNKS = T // T_CHUNK
+VECTOR_CHUNKS = 2
+TILES = T // P
+R_GROUPS = [2,2,2,2]
+OUT_GROUPS = [2,2,2,2]
+
+
+def tile_mix_outl_tm_res_kernel(tc, x, w8_words, w8_scales, w4_words, w4_scales, r, out):
+    nc = tc.nc
+
+    with ExitStack() as ctx:
+        keep = ctx.enter_context(tc.tile_pool(name="keep", bufs=1))
+        psum = ctx.enter_context(tc.psum_pool(name="psum", bufs=8))
+        ctx.enter_context(tc.manual_schedule())
+
+        w_scales = keep.tile([P, PASSES, N], U8, align_bytes=64)
+        w8 = keep.tile([P, N], U32, align_bytes=64)
+        w4 = keep.tile([P, 2 * N], U8, align_bytes=64)
+        x_raw = [keep.tile([P, PACK, T], F32, name="x_raw%d" % g) for g in range(PASSES)]
+        x_codes = [keep.tile([P, T], U32, align_bytes=64, name="x_codes%d" % g) for g in range(PASSES)]
+        x_scales = [keep.tile([P, T], U8, align_bytes=64, name="x_scales%d" % g) for g in range(PASSES)]
+        r_sb = keep.tile([P, TILES, N], F32)
+        out_sb = keep.tile([P, TILES, N], F32)
+        r_tiles = r.rearrange("(i p) n -> p i n", p=P)
+        out_tiles = out.rearrange("(i p) n -> p i n", p=P)
+
+        def load_x(g):
+            rows = x[g * K_PASS : (g + 1) * K_PASS, :]
+            nc.sync.dma_start(out=x_raw[g][:], in_=rows.rearrange("(p j) t -> p j t", j=PACK))
+
+        def load_scales(queue, g):
+            rows = (w8_scales, w4_scales)[g][0].rearrange("(q j) n -> j q n", j=4)
+            for j in range(4):
+                queue.dma_start(out=w_scales[j:P:32, g, :].bitcast(I32), in_=rows[j].bitcast(I32))
+
+        def load_words():
+            nc.sync.dma_start(out=w8[:].bitcast(I32), in_=w8_words[0].rearrange("p n j -> p (n j)").bitcast(I32))
+            nc.sync.dma_start(out=w4[:].bitcast(I32), in_=w4_words[0].bitcast(I32))
+
+        nc.vector.memset(w_scales[:].rearrange("p g n -> p (g n)").bitcast(I32), 0)
+        load_x(0)
+        load_x(1)
+        load_words()
+        load_scales(nc.gpsimd, 0)
+        load_scales(nc.gpsimd, 1)
+        first = 0
+        for count in R_GROUPS:
+            nc.sync.dma_start(out=r_sb[:, first : first + count, :], in_=r_tiles[:, first : first + count, :])
+            first += count
+
+        for g in range(PASSES):
+            grouped = []
+            for c in range(CHUNKS):
+                cols = slice(c * T_CHUNK, (c + 1) * T_CHUNK)
+                chunk = keep.tile([P, T_CHUNK, PACK], BF16, align_bytes=64, name="grouped%d_%d" % (g, c))
+                source = x_raw[g][:, :, cols].rearrange("p j t -> p t j")
+                if c < VECTOR_CHUNKS:
+                    nc.vector.tensor_copy(out=chunk[:], in_=source)
+                else:
+                    nc.scalar.copy(out=chunk[:], in_=source)
+                grouped.append(chunk)
+            for c in range(CHUNKS):
+                cols = slice(c * T_CHUNK, (c + 1) * T_CHUNK)
+                nc.vector.quantize_mx(
+                    out=x_codes[g][:, cols].bitcast(FP8X4),
+                    scales=x_scales[g][:, cols],
+                    in_=grouped[c][:].rearrange("p t j -> p (t j)"),
+                )
+
+        first = 0
+        for count in OUT_GROUPS:
+            for i in range(first, first + count):
+                rows = slice(i * P, (i + 1) * P)
+                banks = []
+                for h in range(N // N_TILE):
+                    bank = psum.tile([P, N_TILE], F32, name="bank")
+                    banks.append(bank)
+                for g in range(PASSES):
+                    for h in range(N // N_TILE):
+                        cols = slice(h * N_TILE, (h + 1) * N_TILE)
+                        if g == 0:
+                            moving = w8[:, cols].bitcast(FP8X4)
+                        else:
+                            moving = w4[:, 2 * cols.start : 2 * cols.stop].bitcast(FP4X4)
+                        nc.tensor.matmul_mx(
+                            out=banks[h][:],
+                            lhsT=x_codes[g][:, rows].bitcast(FP8X4),
+                            lhsT_scale=x_scales[g][:, rows],
+                            rhs=moving,
+                            rhs_scale=w_scales[:, g, cols],
+                            start=(g == 0),
+                            stop=(g == PASSES - 1),
+                        )
+                for h in range(N // N_TILE):
+                    cols = slice(h * N_TILE, (h + 1) * N_TILE)
+                    nc.vector.tensor_add(out=out_sb[:, i, cols], in0=banks[h][:], in1=r_sb[:, i, cols])
+            nc.sync.dma_start(out=out_tiles[:, first : first + count, :], in_=out_sb[:, first : first + count, :])
+            first += count

@@ -60,10 +60,10 @@ def tile_mix_outl_tm_res_kernel(tc, x, w8_words, w8_scales, w4_words, w4_scales,
 
         nc.vector.memset(w_scales[:].rearrange("p g n -> p (g n)").bitcast(I32), 0)
         load_x(0)
+        load_scales(nc.sync, 0)
         load_x(1)
         load_words()
-        load_scales(nc.gpsimd, 0)
-        load_scales(nc.gpsimd, 1)
+        load_scales(nc.sync, 1)
         first = 0
         for count in R_GROUPS:
             nc.sync.dma_start(out=r_sb[:, first : first + count, :], in_=r_tiles[:, first : first + count, :])

@@ -18,12 +18,11 @@ PACK = 4
 K_PASS = P * PACK
 PASSES = K // K_PASS
 N_TILE = 512
-T_CHUNK = 256
-CHUNKS = T // T_CHUNK
-VECTOR_CHUNKS = 2
+RUN = 4
+VECTOR_COLUMNS = 64
 TILES = T // P
 R_GROUPS = [2,2,2,2]
-OUT_GROUPS = [2,2,2,2]
+OUT_GROUPS = [3,3,2]
 
 
 def tile_mix_outl_tm_res_kernel(tc, x, w8_words, w8_scales, w4_words, w4_scales, r, out):
@@ -42,8 +41,8 @@ def tile_mix_outl_tm_res_kernel(tc, x, w8_words, w8_scales, w4_words, w4_scales,
         x_scales = [keep.tile([P, T], U8, align_bytes=64, name="x_scales%d" % g) for g in range(PASSES)]
         r_sb = keep.tile([P, TILES, N], F32)
         out_sb = keep.tile([P, TILES, N], F32)
-        r_tiles = r.rearrange("(i p) n -> p i n", p=P)
-        out_tiles = out.rearrange("(i p) n -> p i n", p=P)
+        r_tiles = r.rearrange("(p i) n -> p i n", i=TILES)
+        out_tiles = out.rearrange("(p i) n -> p i n", i=TILES)
 
         def load_x(g):
             rows = x[g * K_PASS : (g + 1) * K_PASS, :]
@@ -71,21 +70,20 @@ def tile_mix_outl_tm_res_kernel(tc, x, w8_words, w8_scales, w4_words, w4_scales,
 
         for g in range(PASSES):
             grouped = []
-            for c in range(CHUNKS):
-                cols = slice(c * T_CHUNK, (c + 1) * T_CHUNK)
-                chunk = keep.tile([P, T_CHUNK, PACK], BF16, align_bytes=64, name="grouped%d_%d" % (g, c))
-                source = x_raw[g][:, :, cols].rearrange("p j t -> p t j")
-                if c < VECTOR_CHUNKS:
-                    nc.vector.tensor_copy(out=chunk[:], in_=source)
-                else:
-                    nc.scalar.copy(out=chunk[:], in_=source)
+            by_tile = x_raw[g][:].rearrange("p j (m i) -> p m i j", i=TILES)
+            for c in range(TILES // RUN):
+                chunk = keep.tile([P, RUN, P, PACK], BF16, align_bytes=64, name="grouped%d_%d" % (g, c))
+                target = chunk[:].rearrange("p i m j -> p m i j")
+                source = by_tile[:, :, c * RUN : (c + 1) * RUN, :]
+                nc.vector.tensor_copy(out=target[:, :VECTOR_COLUMNS], in_=source[:, :VECTOR_COLUMNS])
+                nc.scalar.copy(out=target[:, VECTOR_COLUMNS:], in_=source[:, VECTOR_COLUMNS:])
                 grouped.append(chunk)
-            for c in range(CHUNKS):
-                cols = slice(c * T_CHUNK, (c + 1) * T_CHUNK)
+            for c in range(TILES // RUN):
+                cols = slice(c * RUN * P, (c + 1) * RUN * P)
                 nc.vector.quantize_mx(
                     out=x_codes[g][:, cols].bitcast(FP8X4),
                     scales=x_scales[g][:, cols],
-                    in_=grouped[c][:].rearrange("p t j -> p (t j)"),
+                    in_=grouped[c][:].rearrange("p i m j -> p (i m j)"),
                 )
 
         first = 0

@@ -19,6 +19,7 @@ K_PASS = P * PACK
 PASSES = K // K_PASS
 N_TILE = 512
 RUN = 4
+PLANE_START = (4, 0)
 VECTOR_COLUMNS = 64
 TILES = T // P
 R_GROUPS = [2,2,2,2]
@@ -33,7 +34,7 @@ def tile_mix_outl_tm_res_kernel(tc, x, w8_words, w8_scales, w4_words, w4_scales,
         psum = ctx.enter_context(tc.psum_pool(name="psum", bufs=8))
         ctx.enter_context(tc.manual_schedule())
 
-        w_scales = keep.tile([P, PASSES, N], U8, align_bytes=64)
+        w_scales = keep.tile([P, N], U8, align_bytes=64)
         w8 = keep.tile([P, N], U32, align_bytes=64)
         w4 = keep.tile([P, 2 * N], U8, align_bytes=64)
         x_raw = [keep.tile([P, PACK, T], F32, name="x_raw%d" % g) for g in range(PASSES)]
@@ -51,13 +52,13 @@ def tile_mix_outl_tm_res_kernel(tc, x, w8_words, w8_scales, w4_words, w4_scales,
         def load_scales(queue, g):
             rows = (w8_scales, w4_scales)[g][0].rearrange("(q j) n -> j q n", j=4)
             for j in range(4):
-                queue.dma_start(out=w_scales[j:P:32, g, :].bitcast(I32), in_=rows[j].bitcast(I32))
+                queue.dma_start(out=w_scales[PLANE_START[g] + j : P : 32, :].bitcast(I32), in_=rows[j].bitcast(I32))
 
         def load_words():
             nc.sync.dma_start(out=w8[:].bitcast(I32), in_=w8_words[0].rearrange("p n j -> p (n j)").bitcast(I32))
             nc.sync.dma_start(out=w4[:].bitcast(I32), in_=w4_words[0].bitcast(I32))
 
-        nc.vector.memset(w_scales[:].rearrange("p g n -> p (g n)").bitcast(I32), 0)
+        nc.vector.memset(w_scales[:].bitcast(I32), 0)
         load_x(0)
         load_scales(nc.sync, 0)
         load_x(1)
@@ -106,7 +107,7 @@ def tile_mix_outl_tm_res_kernel(tc, x, w8_words, w8_scales, w4_words, w4_scales,
                             lhsT=x_codes[g][:, rows].bitcast(FP8X4),
                             lhsT_scale=x_scales[g][:, rows],
                             rhs=moving,
-                            rhs_scale=w_scales[:, g, cols],
+                            rhs_scale=w_scales[PLANE_START[g] :, cols],
                             start=(g == 0),
                             stop=(g == PASSES - 1),
                         )

@@ -20,10 +20,10 @@ PASSES = K // K_PASS
 N_TILE = 512
 RUN = 4
 PLANE_START = (4, 0)
-VECTOR_COLUMNS = 64
+OPEN_TILES = 4
 TILES = T // P
 R_GROUPS = [2,2,2,2]
-OUT_GROUPS = [3,3,2]
+OUT_GROUPS = [2,2,2,2]
 
 
 def tile_mix_outl_tm_res_kernel(tc, x, w8_words, w8_scales, w4_words, w4_scales, r, out):
@@ -34,7 +34,7 @@ def tile_mix_outl_tm_res_kernel(tc, x, w8_words, w8_scales, w4_words, w4_scales,
         psum = ctx.enter_context(tc.psum_pool(name="psum", bufs=8))
         ctx.enter_context(tc.manual_schedule())
 
-        w_scales = keep.tile([P, N], U8, align_bytes=64)
+        w_scales = [keep.tile([P, N], U8, align_bytes=64, name="w_scales%d" % g) for g in range(PASSES)]
         w8 = keep.tile([P, N], U32, align_bytes=64)
         w4 = keep.tile([P, 2 * N], U8, align_bytes=64)
         x_raw = [keep.tile([P, PACK, T], F32, name="x_raw%d" % g) for g in range(PASSES)]
@@ -52,34 +52,28 @@ def tile_mix_outl_tm_res_kernel(tc, x, w8_words, w8_scales, w4_words, w4_scales,
         def load_scales(queue, g):
             rows = (w8_scales, w4_scales)[g][0].rearrange("(q j) n -> j q n", j=4)
             for j in range(4):
-                queue.dma_start(out=w_scales[PLANE_START[g] + j : P : 32, :].bitcast(I32), in_=rows[j].bitcast(I32))
+                queue.dma_start(out=w_scales[g][PLANE_START[g] + j : P : 32, :].bitcast(I32), in_=rows[j].bitcast(I32))
 
-        def load_words():
-            nc.sync.dma_start(out=w8[:].bitcast(I32), in_=w8_words[0].rearrange("p n j -> p (n j)").bitcast(I32))
-            nc.sync.dma_start(out=w4[:].bitcast(I32), in_=w4_words[0].bitcast(I32))
-
-        nc.vector.memset(w_scales[:].bitcast(I32), 0)
         load_x(0)
         load_scales(nc.sync, 0)
+        nc.sync.dma_start(out=w8[:].bitcast(I32), in_=w8_words[0].rearrange("p n j -> p (n j)").bitcast(I32))
         load_x(1)
-        load_words()
+        nc.sync.dma_start(out=w4[:].bitcast(I32), in_=w4_words[0].bitcast(I32))
         load_scales(nc.sync, 1)
         first = 0
         for count in R_GROUPS:
             nc.sync.dma_start(out=r_sb[:, first : first + count, :], in_=r_tiles[:, first : first + count, :])
             first += count
 
-        for g in range(PASSES):
-            grouped = []
+        def quantize_x(g):
             by_tile = x_raw[g][:].rearrange("p j (m i) -> p m i j", i=TILES)
-            for c in range(TILES // RUN):
-                chunk = keep.tile([P, RUN, P, PACK], BF16, align_bytes=64, name="grouped%d_%d" % (g, c))
-                target = chunk[:].rearrange("p i m j -> p m i j")
-                source = by_tile[:, :, c * RUN : (c + 1) * RUN, :]
-                nc.vector.tensor_copy(out=target[:, :VECTOR_COLUMNS], in_=source[:, :VECTOR_COLUMNS])
-                nc.scalar.copy(out=target[:, VECTOR_COLUMNS:], in_=source[:, VECTOR_COLUMNS:])
-                grouped.append(chunk)
-            for c in range(TILES // RUN):
+            grouped = [keep.tile([P, RUN, P, PACK], BF16, align_bytes=64, name="grouped%d_%d" % (g, c)) for c in range(2)]
+
+            def interleave(copy, c, cols):
+                target = grouped[c][:].rearrange("p i m j -> p m i j")
+                copy(out=target[:, cols], in_=by_tile[:, cols, c * RUN : (c + 1) * RUN, :])
+
+            def quantize(c):
                 cols = slice(c * RUN * P, (c + 1) * RUN * P)
                 nc.vector.quantize_mx(
                     out=x_codes[g][:, cols].bitcast(FP8X4),
@@ -87,30 +81,46 @@ def tile_mix_outl_tm_res_kernel(tc, x, w8_words, w8_scales, w4_words, w4_scales,
                     in_=grouped[c][:].rearrange("p i m j -> p (i m j)"),
                 )
 
+            interleave(nc.vector.tensor_copy, 0, slice(0, 84))
+            interleave(nc.scalar.copy, 0, slice(84, P))
+            interleave(nc.scalar.copy, 1, slice(72, P))
+            interleave(nc.vector.tensor_copy, 1, slice(0, 32))
+            quantize(0)
+            interleave(nc.vector.tensor_copy, 1, slice(32, 72))
+            quantize(1)
+
+        def multiply(g, i, banks):
+            rows = slice(i * P, (i + 1) * P)
+            for h in range(N // N_TILE):
+                cols = slice(h * N_TILE, (h + 1) * N_TILE)
+                if g == 0:
+                    moving = w8[:, cols].bitcast(FP8X4)
+                else:
+                    moving = w4[:, 2 * cols.start : 2 * cols.stop].bitcast(FP4X4)
+                nc.tensor.matmul_mx(
+                    out=banks[h][:],
+                    lhsT=x_codes[g][:, rows].bitcast(FP8X4),
+                    lhsT_scale=x_scales[g][:, rows],
+                    rhs=moving,
+                    rhs_scale=w_scales[g][PLANE_START[g] :, cols],
+                    start=(g == 0),
+                    stop=(g == PASSES - 1),
+                )
+
+        def open_tile(i):
+            banks = [psum.tile([P, N_TILE], F32, name="bank") for h in range(N // N_TILE)]
+            multiply(0, i, banks)
+            return banks
+
+        quantize_x(0)
+        opened = [open_tile(i) for i in range(OPEN_TILES)]
+        quantize_x(1)
+
         first = 0
         for count in OUT_GROUPS:
             for i in range(first, first + count):
-                rows = slice(i * P, (i + 1) * P)
-                banks = []
-                for h in range(N // N_TILE):
-                    bank = psum.tile([P, N_TILE], F32, name="bank")
-                    banks.append(bank)
-                for g in range(PASSES):
-                    for h in range(N // N_TILE):
-                        cols = slice(h * N_TILE, (h + 1) * N_TILE)
-                        if g == 0:
-                            moving = w8[:, cols].bitcast(FP8X4)
-                        else:
-                            moving = w4[:, 2 * cols.start : 2 * cols.stop].bitcast(FP4X4)
-                        nc.tensor.matmul_mx(
-                            out=banks[h][:],
-                            lhsT=x_codes[g][:, rows].bitcast(FP8X4),
-                            lhsT_scale=x_scales[g][:, rows],
-                            rhs=moving,
-                            rhs_scale=w_scales[PLANE_START[g] :, cols],
-                            start=(g == 0),
-                            stop=(g == PASSES - 1),
-                        )
+                banks = opened[i] if i < OPEN_TILES else open_tile(i)
+                multiply(1, i, banks)
                 for h in range(N // N_TILE):
                     cols = slice(h * N_TILE, (h + 1) * N_TILE)
                     nc.vector.tensor_add(out=out_sb[:, i, cols], in0=banks[h][:], in1=r_sb[:, i, cols])

@@ -21,6 +21,7 @@ N_TILE = 512
 RUN = 4
 PLANE_START = (4, 0)
 OPEN_TILES = 4
+DMA_ALIGN = 4096
 TILES = T // P
 R_GROUPS = [2,2,2,2]
 OUT_GROUPS = [2,2,2,2]
@@ -34,14 +35,14 @@ def tile_mix_outl_tm_res_kernel(tc, x, w8_words, w8_scales, w4_words, w4_scales,
         psum = ctx.enter_context(tc.psum_pool(name="psum", bufs=8))
         ctx.enter_context(tc.manual_schedule())
 
-        w_scales = [keep.tile([P, N], U8, align_bytes=64, name="w_scales%d" % g) for g in range(PASSES)]
-        w8 = keep.tile([P, N], U32, align_bytes=64)
-        w4 = keep.tile([P, 2 * N], U8, align_bytes=64)
-        x_raw = [keep.tile([P, PACK, T], F32, name="x_raw%d" % g) for g in range(PASSES)]
+        w_scales = [keep.tile([P, N], U8, align_bytes=DMA_ALIGN, name="w_scales%d" % g) for g in range(PASSES)]
+        w8 = keep.tile([P, N], U32, align_bytes=DMA_ALIGN)
+        w4 = keep.tile([P, 2 * N], U8, align_bytes=DMA_ALIGN)
+        x_raw = [keep.tile([P, PACK, T], F32, align_bytes=DMA_ALIGN, name="x_raw%d" % g) for g in range(PASSES)]
         x_codes = [keep.tile([P, T], U32, align_bytes=64, name="x_codes%d" % g) for g in range(PASSES)]
         x_scales = [keep.tile([P, T], U8, align_bytes=64, name="x_scales%d" % g) for g in range(PASSES)]
-        r_sb = keep.tile([P, TILES, N], F32)
-        out_sb = keep.tile([P, TILES, N], F32)
+        r_sb = keep.tile([P, TILES, N], F32, align_bytes=DMA_ALIGN)
+        out_sb = keep.tile([P, TILES, N], F32, align_bytes=DMA_ALIGN)
         r_tiles = r.rearrange("(p i) n -> p i n", i=TILES)
         out_tiles = out.rearrange("(p i) n -> p i n", i=TILES)
 

@@ -1,4 +1,5 @@
 from contextlib import ExitStack
+from itertools import accumulate
 
 import concourse.mybir as mybir
 
@@ -23,8 +24,9 @@ PLANE_START = (4, 0)
 OPEN_TILES = 4
 DMA_ALIGN = 4096
 TILES = T // P
-R_GROUPS = [2,2,2,2]
-OUT_GROUPS = [2,2,2,2]
+BANKS = TILES * (N // N_TILE)
+R_GROUPS = (3, 3, 3, 3, 4)
+OUT_GROUPS = (3, 3, 3, 3, 2, 2)
 
 
 def tile_mix_outl_tm_res_kernel(tc, x, w8_words, w8_scales, w4_words, w4_scales, r, out):
@@ -41,10 +43,10 @@ def tile_mix_outl_tm_res_kernel(tc, x, w8_words, w8_scales, w4_words, w4_scales,
         x_raw = [keep.tile([P, PACK, T], F32, align_bytes=DMA_ALIGN, name="x_raw%d" % g) for g in range(PASSES)]
         x_codes = [keep.tile([P, T], U32, align_bytes=64, name="x_codes%d" % g) for g in range(PASSES)]
         x_scales = [keep.tile([P, T], U8, align_bytes=64, name="x_scales%d" % g) for g in range(PASSES)]
-        r_sb = keep.tile([P, TILES, N], F32, align_bytes=DMA_ALIGN)
-        out_sb = keep.tile([P, TILES, N], F32, align_bytes=DMA_ALIGN)
-        r_tiles = r.rearrange("(p i) n -> p i n", i=TILES)
-        out_tiles = out.rearrange("(p i) n -> p i n", i=TILES)
+        r_sb = keep.tile([P, BANKS, N_TILE], F32, align_bytes=DMA_ALIGN)
+        out_sb = keep.tile([P, BANKS, N_TILE], F32, align_bytes=DMA_ALIGN)
+        r_tiles = r.rearrange("(p i) (h n) -> p (i h) n", i=TILES, n=N_TILE)
+        out_tiles = out.rearrange("(p i) (h n) -> p (i h) n", i=TILES, n=N_TILE)
 
         def load_x(g):
             rows = x[g * K_PASS : (g + 1) * K_PASS, :]
@@ -117,13 +119,13 @@ def tile_mix_outl_tm_res_kernel(tc, x, w8_words, w8_scales, w4_words, w4_scales,
         opened = [open_tile(i) for i in range(OPEN_TILES)]
         quantize_x(1)
 
-        first = 0
-        for count in OUT_GROUPS:
-            for i in range(first, first + count):
-                banks = opened[i] if i < OPEN_TILES else open_tile(i)
-                multiply(1, i, banks)
-                for h in range(N // N_TILE):
-                    cols = slice(h * N_TILE, (h + 1) * N_TILE)
-                    nc.vector.tensor_add(out=out_sb[:, i, cols], in0=banks[h][:], in1=r_sb[:, i, cols])
-            nc.sync.dma_start(out=out_tiles[:, first : first + count, :], in_=out_sb[:, first : first + count, :])
-            first += count
+        ends = list(accumulate(OUT_GROUPS))
+        for i in range(TILES):
+            banks = opened[i] if i < OPEN_TILES else open_tile(i)
+            multiply(1, i, banks)
+            for h in range(N // N_TILE):
+                b = i * (N // N_TILE) + h
+                nc.vector.tensor_add(out=out_sb[:, b, :], in0=banks[h][:], in1=r_sb[:, b, :])
+                if b + 1 in ends:
+                    first = b + 1 - OUT_GROUPS[ends.index(b + 1)]
+                    nc.sync.dma_start(out=out_tiles[:, first : b + 1, :], in_=out_sb[:, first : b + 1, :])

@@ -25,8 +25,8 @@ OPEN_TILES = 4
 DMA_ALIGN = 4096
 TILES = T // P
 BANKS = TILES * (N // N_TILE)
-R_GROUPS = (3, 3, 3, 3, 4)
-OUT_GROUPS = (3, 3, 3, 3, 2, 2)
+R_GROUPS = (5, 5, 6)
+OUT_GROUPS = (6, 5, 5)
 
 
 def tile_mix_outl_tm_res_kernel(tc, x, w8_words, w8_scales, w4_words, w4_scales, r, out):
@@ -52,17 +52,18 @@ def tile_mix_outl_tm_res_kernel(tc, x, w8_words, w8_scales, w4_words, w4_scales,
             rows = x[g * K_PASS : (g + 1) * K_PASS, :]
             nc.sync.dma_start(out=x_raw[g][:], in_=rows.rearrange("(p j) t -> p j t", j=PACK))
 
-        def load_scales(queue, g):
+        def load_scales(queue, g, which, **how):
             rows = (w8_scales, w4_scales)[g][0].rearrange("(q j) n -> j q n", j=4)
-            for j in range(4):
-                queue.dma_start(out=w_scales[g][PLANE_START[g] + j : P : 32, :].bitcast(I32), in_=rows[j].bitcast(I32))
+            for j in which:
+                queue.dma_start(out=w_scales[g][PLANE_START[g] + j : P : 32, :].bitcast(I32), in_=rows[j].bitcast(I32), **how)
 
+        load_scales(nc.gpsimd, 1, range(2), max_dma_last_dim=N // 2)
         load_x(0)
-        load_scales(nc.sync, 0)
+        load_scales(nc.sync, 0, range(4))
         nc.sync.dma_start(out=w8[:].bitcast(I32), in_=w8_words[0].rearrange("p n j -> p (n j)").bitcast(I32))
         load_x(1)
         nc.sync.dma_start(out=w4[:].bitcast(I32), in_=w4_words[0].bitcast(I32))
-        load_scales(nc.sync, 1)
+        load_scales(nc.sync, 1, range(2, 4))
         first = 0
         for count in R_GROUPS:
             nc.sync.dma_start(out=r_sb[:, first : first + count, :], in_=r_tiles[:, first : first + count, :])

@@ -57,13 +57,16 @@ def tile_mix_outl_tm_res_kernel(tc, x, w8_words, w8_scales, w4_words, w4_scales,
             for j in which:
                 queue.dma_start(out=w_scales[g][PLANE_START[g] + j : P : 32, :].bitcast(I32), in_=rows[j].bitcast(I32), **how)
 
-        load_scales(nc.gpsimd, 1, range(2), max_dma_last_dim=N // 2)
+        load_scales(nc.gpsimd, 0, range(2), max_dma_last_dim=N // 2)
         load_x(0)
-        load_scales(nc.sync, 0, range(4))
+        for j in range(2):
+            load_scales(nc.sync, 0, [2 + j])
+            load_scales(nc.sync, 1, [j])
         nc.sync.dma_start(out=w8[:].bitcast(I32), in_=w8_words[0].rearrange("p n j -> p (n j)").bitcast(I32))
         load_x(1)
+        load_scales(nc.sync, 1, [2])
         nc.sync.dma_start(out=w4[:].bitcast(I32), in_=w4_words[0].bitcast(I32))
-        load_scales(nc.sync, 1, range(2, 4))
+        load_scales(nc.sync, 1, [3])
         first = 0
         for count in R_GROUPS:
             nc.sync.dma_start(out=r_sb[:, first : first + count, :], in_=r_tiles[:, first : first + count, :])

@@ -59,10 +59,10 @@ def tile_mix_outl_tm_res_kernel(tc, x, w8_words, w8_scales, w4_words, w4_scales,
 
         load_scales(nc.gpsimd, 0, range(2), max_dma_last_dim=N // 2)
         load_x(0)
+        nc.scalar.dma_start(out=w8[:].bitcast(I32), in_=w8_words[0].rearrange("p n j -> p (n j)").bitcast(I32))
         for j in range(2):
             load_scales(nc.sync, 0, [2 + j])
             load_scales(nc.sync, 1, [j])
-        nc.sync.dma_start(out=w8[:].bitcast(I32), in_=w8_words[0].rearrange("p n j -> p (n j)").bitcast(I32))
         load_x(1)
         load_scales(nc.sync, 1, [2])
         nc.sync.dma_start(out=w4[:].bitcast(I32), in_=w4_words[0].bitcast(I32))

@@ -61,12 +61,12 @@ def tile_mix_outl_tm_res_kernel(tc, x, w8_words, w8_scales, w4_words, w4_scales,
         load_x(0)
         nc.scalar.dma_start(out=w8[:].bitcast(I32), in_=w8_words[0].rearrange("p n j -> p (n j)").bitcast(I32))
         for j in range(2):
-            load_scales(nc.sync, 0, [2 + j])
-            load_scales(nc.sync, 1, [j])
+            load_scales(nc.scalar, 0, [2 + j])
+            load_scales(nc.scalar, 1, [j])
         load_x(1)
-        load_scales(nc.sync, 1, [2])
-        nc.sync.dma_start(out=w4[:].bitcast(I32), in_=w4_words[0].bitcast(I32))
+        load_scales(nc.scalar, 1, [2])
         load_scales(nc.sync, 1, [3])
+        nc.sync.dma_start(out=w4[:].bitcast(I32), in_=w4_words[0].bitcast(I32))
         first = 0
         for count in R_GROUPS:
             nc.sync.dma_start(out=r_sb[:, first : first + count, :], in_=r_tiles[:, first : first + count, :])

@@ -23,6 +23,7 @@ RUN = 4
 PLANE_START = (4, 0)
 OPEN_TILES = 4
 DMA_ALIGN = 4096
+STREAM_ALIGN = 16384
 TILES = T // P
 BANKS = TILES * (N // N_TILE)
 R_GROUPS = (5, 5, 6)
@@ -34,17 +35,18 @@ def tile_mix_outl_tm_res_kernel(tc, x, w8_words, w8_scales, w4_words, w4_scales,
 
     with ExitStack() as ctx:
         keep = ctx.enter_context(tc.tile_pool(name="keep", bufs=1))
+        stream = ctx.enter_context(tc.tile_pool(name="stream", bufs=1))
         psum = ctx.enter_context(tc.psum_pool(name="psum", bufs=8))
         ctx.enter_context(tc.manual_schedule())
 
         w_scales = [keep.tile([P, N], U8, align_bytes=DMA_ALIGN, name="w_scales%d" % g) for g in range(PASSES)]
         w8 = keep.tile([P, N], U32, align_bytes=DMA_ALIGN)
         w4 = keep.tile([P, 2 * N], U8, align_bytes=DMA_ALIGN)
-        x_raw = [keep.tile([P, PACK, T], F32, align_bytes=DMA_ALIGN, name="x_raw%d" % g) for g in range(PASSES)]
+        x_raw = [stream.tile([P, PACK, T], F32, align_bytes=STREAM_ALIGN, name="x_raw%d" % g) for g in range(PASSES)]
         x_codes = [keep.tile([P, T], U32, align_bytes=64, name="x_codes%d" % g) for g in range(PASSES)]
         x_scales = [keep.tile([P, T], U8, align_bytes=64, name="x_scales%d" % g) for g in range(PASSES)]
-        r_sb = keep.tile([P, BANKS, N_TILE], F32, align_bytes=DMA_ALIGN)
-        out_sb = keep.tile([P, BANKS, N_TILE], F32, align_bytes=DMA_ALIGN)
+        r_sb = stream.tile([P, BANKS, N_TILE], F32, align_bytes=STREAM_ALIGN)
+        out_sb = stream.tile([P, BANKS, N_TILE], F32, align_bytes=STREAM_ALIGN)
         r_tiles = r.rearrange("(p i) (h n) -> p (i h) n", i=TILES, n=N_TILE)
         out_tiles = out.rearrange("(p i) (h n) -> p (i h) n", i=TILES, n=N_TILE)
 

@@ -19,13 +19,14 @@ PACK = 4
 K_PASS = P * PACK
 PASSES = K // K_PASS
 N_TILE = 512
+HALVES = N // N_TILE
+TILES = T // P
+BANKS = TILES * HALVES
 RUN = 4
 PLANE_START = (4, 0)
 OPEN_TILES = 4
 DMA_ALIGN = 4096
-STREAM_ALIGN = 16384
-TILES = T // P
-BANKS = TILES * (N // N_TILE)
+X_PIECE = 8192
 R_GROUPS = (5, 5, 6)
 OUT_GROUPS = (6, 5, 5)
 
@@ -35,44 +36,36 @@ def tile_mix_outl_tm_res_kernel(tc, x, w8_words, w8_scales, w4_words, w4_scales,
 
     with ExitStack() as ctx:
         keep = ctx.enter_context(tc.tile_pool(name="keep", bufs=1))
-        stream = ctx.enter_context(tc.tile_pool(name="stream", bufs=1))
         psum = ctx.enter_context(tc.psum_pool(name="psum", bufs=8))
         ctx.enter_context(tc.manual_schedule())
 
-        w_scales = [keep.tile([P, N], U8, align_bytes=DMA_ALIGN, name="w_scales%d" % g) for g in range(PASSES)]
         w8 = keep.tile([P, N], U32, align_bytes=DMA_ALIGN)
         w4 = keep.tile([P, 2 * N], U8, align_bytes=DMA_ALIGN)
-        x_raw = [stream.tile([P, PACK, T], F32, align_bytes=STREAM_ALIGN, name="x_raw%d" % g) for g in range(PASSES)]
+        w_scales = [keep.tile([P, N], U8, align_bytes=DMA_ALIGN, name="w_scales%d" % g) for g in range(PASSES)]
+        x_raw = [keep.tile([P, PACK, T], F32, align_bytes=DMA_ALIGN, name="x_raw%d" % g) for g in range(PASSES)]
         x_codes = [keep.tile([P, T], U32, align_bytes=64, name="x_codes%d" % g) for g in range(PASSES)]
         x_scales = [keep.tile([P, T], U8, align_bytes=64, name="x_scales%d" % g) for g in range(PASSES)]
-        r_sb = stream.tile([P, BANKS, N_TILE], F32, align_bytes=STREAM_ALIGN)
-        out_sb = stream.tile([P, BANKS, N_TILE], F32, align_bytes=STREAM_ALIGN)
-        r_tiles = r.rearrange("(p i) (h n) -> p (i h) n", i=TILES, n=N_TILE)
-        out_tiles = out.rearrange("(p i) (h n) -> p (i h) n", i=TILES, n=N_TILE)
+        r_sb = keep.tile([P, BANKS, N_TILE], F32, align_bytes=DMA_ALIGN)
+        out_sb = keep.tile([P, BANKS, N_TILE], F32, align_bytes=DMA_ALIGN)
+        r_banks = r.rearrange("(p i) (h n) -> p (i h) n", i=TILES, n=N_TILE)
+        out_banks = out.rearrange("(p i) (h n) -> p (i h) n", i=TILES, n=N_TILE)
 
-        def load_x(g):
+        for g in range(PASSES):
             rows = x[g * K_PASS : (g + 1) * K_PASS, :]
-            nc.sync.dma_start(out=x_raw[g][:], in_=rows.rearrange("(p j) t -> p j t", j=PACK))
+            nc.sync.dma_start(out=x_raw[g][:], in_=rows.rearrange("(p j) t -> p j t", j=PACK), max_dma_last_dim=X_PIECE)
+        for count, end in zip(R_GROUPS, accumulate(R_GROUPS)):
+            nc.sync.dma_start(out=r_sb[:, end - count : end, :], in_=r_banks[:, end - count : end, :])
 
-        def load_scales(queue, g, which, **how):
+        words = (w8_words[0].rearrange("p n j -> p (n j)"), w4_words[0])
+        for g in range(PASSES):
+            nc.gpsimd.dma_start(out=(w8, w4)[g][:].bitcast(I32), in_=words[g].bitcast(I32))
             rows = (w8_scales, w4_scales)[g][0].rearrange("(q j) n -> j q n", j=4)
-            for j in which:
-                queue.dma_start(out=w_scales[g][PLANE_START[g] + j : P : 32, :].bitcast(I32), in_=rows[j].bitcast(I32), **how)
-
-        load_scales(nc.gpsimd, 0, range(2), max_dma_last_dim=N // 2)
-        load_x(0)
-        nc.scalar.dma_start(out=w8[:].bitcast(I32), in_=w8_words[0].rearrange("p n j -> p (n j)").bitcast(I32))
-        for j in range(2):
-            load_scales(nc.scalar, 0, [2 + j])
-            load_scales(nc.scalar, 1, [j])
-        load_x(1)
-        load_scales(nc.scalar, 1, [2])
-        load_scales(nc.sync, 1, [3])
-        nc.sync.dma_start(out=w4[:].bitcast(I32), in_=w4_words[0].bitcast(I32))
-        first = 0
-        for count in R_GROUPS:
-            nc.sync.dma_start(out=r_sb[:, first : first + count, :], in_=r_tiles[:, first : first + count, :])
-            first += count
+            for j in range(4):
+                nc.gpsimd.dma_start(
+                    out=w_scales[g][PLANE_START[g] + j : P : 32, :].bitcast(I32),
+                    in_=rows[j].bitcast(I32),
+                    max_dma_last_dim=N // 2,
+                )
 
         def quantize_x(g):
             by_tile = x_raw[g][:].rearrange("p j (m i) -> p m i j", i=TILES)
@@ -100,7 +93,7 @@ def tile_mix_outl_tm_res_kernel(tc, x, w8_words, w8_scales, w4_words, w4_scales,
 
         def multiply(g, i, banks):
             rows = slice(i * P, (i + 1) * P)
-            for h in range(N // N_TILE):
+            for h in range(HALVES):
                 cols = slice(h * N_TILE, (h + 1) * N_TILE)
                 if g == 0:
                     moving = w8[:, cols].bitcast(FP8X4)
@@ -117,7 +110,7 @@ def tile_mix_outl_tm_res_kernel(tc, x, w8_words, w8_scales, w4_words, w4_scales,
                 )
 
         def open_tile(i):
-            banks = [psum.tile([P, N_TILE], F32, name="bank") for h in range(N // N_TILE)]
+            banks = [psum.tile([P, N_TILE], F32, name="bank") for h in range(HALVES)]
             multiply(0, i, banks)
             return banks
 
@@ -129,9 +122,9 @@ def tile_mix_outl_tm_res_kernel(tc, x, w8_words, w8_scales, w4_words, w4_scales,
         for i in range(TILES):
             banks = opened[i] if i < OPEN_TILES else open_tile(i)
             multiply(1, i, banks)
-            for h in range(N // N_TILE):
-                b = i * (N // N_TILE) + h
+            for h in range(HALVES):
+                b = i * HALVES + h
                 nc.vector.tensor_add(out=out_sb[:, b, :], in0=banks[h][:], in1=r_sb[:, b, :])
                 if b + 1 in ends:
                     first = b + 1 - OUT_GROUPS[ends.index(b + 1)]
-                    nc.sync.dma_start(out=out_tiles[:, first : b + 1, :], in_=out_sb[:, first : b + 1, :])
+                    nc.sync.dma_start(out=out_banks[:, first : b + 1, :], in_=out_sb[:, first : b + 1, :])

@@ -24,7 +24,7 @@ TILES = T // P
 BANKS = TILES * HALVES
 RUN = 4
 PLANE_START = (4, 0)
-OPEN_TILES = 4
+OPEN_TILES = 3
 DMA_ALIGN = 4096
 X_PIECE = 8192
 R_GROUPS = (5, 5, 6)
@@ -67,29 +67,23 @@ def tile_mix_outl_tm_res_kernel(tc, x, w8_words, w8_scales, w4_words, w4_scales,
                     max_dma_last_dim=N // 2,
                 )
 
-        def quantize_x(g):
+        grouped = [
+            [keep.tile([P, RUN, P, PACK], BF16, align_bytes=64, name="grouped%d_%d" % (g, c)) for c in range(TILES // RUN)]
+            for g in range(PASSES)
+        ]
+
+        def interleave(copy, g, c, cols):
             by_tile = x_raw[g][:].rearrange("p j (m i) -> p m i j", i=TILES)
-            grouped = [keep.tile([P, RUN, P, PACK], BF16, align_bytes=64, name="grouped%d_%d" % (g, c)) for c in range(2)]
+            target = grouped[g][c][:].rearrange("p i m j -> p m i j")
+            copy(out=target[:, cols], in_=by_tile[:, cols, c * RUN : (c + 1) * RUN, :])
 
-            def interleave(copy, c, cols):
-                target = grouped[c][:].rearrange("p i m j -> p m i j")
-                copy(out=target[:, cols], in_=by_tile[:, cols, c * RUN : (c + 1) * RUN, :])
-
-            def quantize(c):
-                cols = slice(c * RUN * P, (c + 1) * RUN * P)
-                nc.vector.quantize_mx(
-                    out=x_codes[g][:, cols].bitcast(FP8X4),
-                    scales=x_scales[g][:, cols],
-                    in_=grouped[c][:].rearrange("p i m j -> p (i m j)"),
-                )
-
-            interleave(nc.vector.tensor_copy, 0, slice(0, 84))
-            interleave(nc.scalar.copy, 0, slice(84, P))
-            interleave(nc.scalar.copy, 1, slice(72, P))
-            interleave(nc.vector.tensor_copy, 1, slice(0, 32))
-            quantize(0)
-            interleave(nc.vector.tensor_copy, 1, slice(32, 72))
-            quantize(1)
+        def quantize(g, c):
+            cols = slice(c * RUN * P, (c + 1) * RUN * P)
+            nc.vector.quantize_mx(
+                out=x_codes[g][:, cols].bitcast(FP8X4),
+                scales=x_scales[g][:, cols],
+                in_=grouped[g][c][:].rearrange("p i m j -> p (i m j)"),
+            )
 
         def multiply(g, i, banks):
             rows = slice(i * P, (i + 1) * P)
@@ -114,17 +108,39 @@ def tile_mix_outl_tm_res_kernel(tc, x, w8_words, w8_scales, w4_words, w4_scales,
             multiply(0, i, banks)
             return banks
 
-        quantize_x(0)
-        opened = [open_tile(i) for i in range(OPEN_TILES)]
-        quantize_x(1)
-
         ends = list(accumulate(OUT_GROUPS))
-        for i in range(TILES):
-            banks = opened[i] if i < OPEN_TILES else open_tile(i)
-            multiply(1, i, banks)
+
+        def add_and_store(i, banks):
             for h in range(HALVES):
                 b = i * HALVES + h
                 nc.vector.tensor_add(out=out_sb[:, b, :], in0=banks[h][:], in1=r_sb[:, b, :])
                 if b + 1 in ends:
                     first = b + 1 - OUT_GROUPS[ends.index(b + 1)]
                     nc.sync.dma_start(out=out_banks[:, first : b + 1, :], in_=out_sb[:, first : b + 1, :])
+
+        def close_tiles(first, opened):
+            for i, banks in enumerate(opened, first):
+                multiply(1, i, banks)
+                add_and_store(i, banks)
+
+        interleave(nc.scalar.copy, 0, 0, slice(0, P))
+        quantize(0, 0)
+        interleave(nc.vector.tensor_copy, 0, 1, slice(0, 64))
+        interleave(nc.scalar.copy, 0, 1, slice(64, P))
+        quantize(0, 1)
+        opened = [open_tile(i) for i in range(OPEN_TILES)]
+
+        interleave(nc.vector.tensor_copy, 1, 0, slice(0, 76))
+        interleave(nc.scalar.copy, 1, 0, slice(76, P))
+        interleave(nc.vector.tensor_copy, 1, 1, slice(0, 32))
+        interleave(nc.scalar.copy, 1, 1, slice(32, P))
+        quantize(1, 0)
+        close_tiles(0, opened)
+        quantize(1, 1)
+
+        banks = open_tile(OPEN_TILES)
+        multiply(1, OPEN_TILES, banks)
+        opened = [open_tile(RUN + i) for i in range(OPEN_TILES)]
+        add_and_store(OPEN_TILES, banks)
+        close_tiles(RUN, opened)
+        close_tiles(TILES - 1, [open_tile(TILES - 1)])

@@ -26,7 +26,7 @@ RUN = 4
 PLANE_START = (4, 0)
 OPEN_TILES = 3
 DMA_ALIGN = 4096
-X_PIECE = 8192
+X_PIECES = (4096, 8192)
 R_GROUPS = (5, 5, 6)
 OUT_GROUPS = (6, 5, 5)
 
@@ -52,7 +52,7 @@ def tile_mix_outl_tm_res_kernel(tc, x, w8_words, w8_scales, w4_words, w4_scales,
 
         for g in range(PASSES):
             rows = x[g * K_PASS : (g + 1) * K_PASS, :]
-            nc.sync.dma_start(out=x_raw[g][:], in_=rows.rearrange("(p j) t -> p j t", j=PACK), max_dma_last_dim=X_PIECE)
+            nc.sync.dma_start(out=x_raw[g][:], in_=rows.rearrange("(p j) t -> p j t", j=PACK), max_dma_last_dim=X_PIECES[g])
         for count, end in zip(R_GROUPS, accumulate(R_GROUPS)):
             nc.sync.dma_start(out=r_sb[:, end - count : end, :], in_=r_banks[:, end - count : end, :])
 

@@ -26,7 +26,7 @@ RUN = 4
 PLANE_START = (4, 0)
 OPEN_TILES = 3
 DMA_ALIGN = 4096
-X_PIECES = (4096, 8192)
+X_PIECE = 4096
 R_GROUPS = (5, 5, 6)
 OUT_GROUPS = (6, 5, 5)
 
@@ -52,13 +52,14 @@ def tile_mix_outl_tm_res_kernel(tc, x, w8_words, w8_scales, w4_words, w4_scales,
 
         for g in range(PASSES):
             rows = x[g * K_PASS : (g + 1) * K_PASS, :]
-            nc.sync.dma_start(out=x_raw[g][:], in_=rows.rearrange("(p j) t -> p j t", j=PACK), max_dma_last_dim=X_PIECES[g])
+            nc.sync.dma_start(out=x_raw[g][:], in_=rows.rearrange("(p j) t -> p j t", j=PACK), max_dma_last_dim=X_PIECE)
         for count, end in zip(R_GROUPS, accumulate(R_GROUPS)):
             nc.sync.dma_start(out=r_sb[:, end - count : end, :], in_=r_banks[:, end - count : end, :])
 
         words = (w8_words[0].rearrange("p n j -> p (n j)"), w4_words[0])
         for g in range(PASSES):
             nc.gpsimd.dma_start(out=(w8, w4)[g][:].bitcast(I32), in_=words[g].bitcast(I32))
+        for g in range(PASSES):
             rows = (w8_scales, w4_scales)[g][0].rearrange("(q j) n -> j q n", j=4)
             for j in range(4):
                 nc.gpsimd.dma_start(

@@ -24,11 +24,11 @@ TILES = T // P
 BANKS = TILES * HALVES
 RUN = 4
 PLANE_START = (4, 0)
-OPEN_TILES = 3
+OPEN_TILES = 4
 DMA_ALIGN = 4096
-X_PIECE = 4096
-R_GROUPS = (5, 5, 6)
-OUT_GROUPS = (6, 5, 5)
+R_GROUPS = (5, 4, 7)
+OUT_GROUPS = (9, 7)
+SECOND_ADDER = (0, 3, 5, 9, 11)
 
 
 def tile_mix_outl_tm_res_kernel(tc, x, w8_words, w8_scales, w4_words, w4_scales, r, out):
@@ -50,41 +50,50 @@ def tile_mix_outl_tm_res_kernel(tc, x, w8_words, w8_scales, w4_words, w4_scales,
         r_banks = r.rearrange("(p i) (h n) -> p (i h) n", i=TILES, n=N_TILE)
         out_banks = out.rearrange("(p i) (h n) -> p (i h) n", i=TILES, n=N_TILE)
 
-        for g in range(PASSES):
+        def load_x(g):
             rows = x[g * K_PASS : (g + 1) * K_PASS, :]
-            nc.sync.dma_start(out=x_raw[g][:], in_=rows.rearrange("(p j) t -> p j t", j=PACK), max_dma_last_dim=X_PIECE)
+            nc.sync.dma_start(out=x_raw[g][:], in_=rows.rearrange("(p j) t -> p j t", j=PACK))
+
+        def load_scales(queue, g, j, **how):
+            rows = (w8_scales, w4_scales)[g][0].rearrange("(q j) n -> j q n", j=4)
+            queue.dma_start(out=w_scales[g][PLANE_START[g] + j : P : 32, :].bitcast(I32), in_=rows[j].bitcast(I32), **how)
+
+        load_scales(nc.gpsimd, 1, 0, max_dma_last_dim=N // 2)
+        load_x(0)
+        nc.scalar.dma_start(out=w8[:].bitcast(I32), in_=w8_words[0].rearrange("p n j -> p (n j)").bitcast(I32))
+        for j in range(4):
+            load_scales(nc.sync, 0, j)
+        load_scales(nc.sync, 1, 1)
+        load_x(1)
+        load_scales(nc.sync, 1, 2)
+        nc.sync.dma_start(out=w4[:].bitcast(I32), in_=w4_words[0].bitcast(I32))
+        load_scales(nc.sync, 1, 3)
         for count, end in zip(R_GROUPS, accumulate(R_GROUPS)):
             nc.sync.dma_start(out=r_sb[:, end - count : end, :], in_=r_banks[:, end - count : end, :])
 
-        words = (w8_words[0].rearrange("p n j -> p (n j)"), w4_words[0])
-        for g in range(PASSES):
-            nc.gpsimd.dma_start(out=(w8, w4)[g][:].bitcast(I32), in_=words[g].bitcast(I32))
-        for g in range(PASSES):
-            rows = (w8_scales, w4_scales)[g][0].rearrange("(q j) n -> j q n", j=4)
-            for j in range(4):
-                nc.gpsimd.dma_start(
-                    out=w_scales[g][PLANE_START[g] + j : P : 32, :].bitcast(I32),
-                    in_=rows[j].bitcast(I32),
-                    max_dma_last_dim=N // 2,
+        def quantize_x(g):
+            by_tile = x_raw[g][:].rearrange("p j (m i) -> p m i j", i=TILES)
+            grouped = [keep.tile([P, RUN, P, PACK], BF16, align_bytes=64, name="grouped%d_%d" % (g, c)) for c in range(2)]
+
+            def interleave(copy, c, cols):
+                target = grouped[c][:].rearrange("p i m j -> p m i j")
+                copy(out=target[:, cols], in_=by_tile[:, cols, c * RUN : (c + 1) * RUN, :])
+
+            def quantize(c):
+                cols = slice(c * RUN * P, (c + 1) * RUN * P)
+                nc.vector.quantize_mx(
+                    out=x_codes[g][:, cols].bitcast(FP8X4),
+                    scales=x_scales[g][:, cols],
+                    in_=grouped[c][:].rearrange("p i m j -> p (i m j)"),
                 )
 
-        grouped = [
-            [keep.tile([P, RUN, P, PACK], BF16, align_bytes=64, name="grouped%d_%d" % (g, c)) for c in range(TILES // RUN)]
-            for g in range(PASSES)
-        ]
-
-        def interleave(copy, g, c, cols):
-            by_tile = x_raw[g][:].rearrange("p j (m i) -> p m i j", i=TILES)
-            target = grouped[g][c][:].rearrange("p i m j -> p m i j")
-            copy(out=target[:, cols], in_=by_tile[:, cols, c * RUN : (c + 1) * RUN, :])
-
-        def quantize(g, c):
-            cols = slice(c * RUN * P, (c + 1) * RUN * P)
-            nc.vector.quantize_mx(
-                out=x_codes[g][:, cols].bitcast(FP8X4),
-                scales=x_scales[g][:, cols],
-                in_=grouped[g][c][:].rearrange("p i m j -> p (i m j)"),
-            )
+            interleave(nc.vector.tensor_copy, 0, slice(0, 84))
+            interleave(nc.scalar.copy, 0, slice(84, P))
+            interleave(nc.scalar.copy, 1, slice(72, P))
+            interleave(nc.vector.tensor_copy, 1, slice(0, 32))
+            quantize(0)
+            interleave(nc.vector.tensor_copy, 1, slice(32, 72))
+            quantize(1)
 
         def multiply(g, i, banks):
             rows = slice(i * P, (i + 1) * P)
@@ -109,39 +118,21 @@ def tile_mix_outl_tm_res_kernel(tc, x, w8_words, w8_scales, w4_words, w4_scales,
             multiply(0, i, banks)
             return banks
 
-        ends = list(accumulate(OUT_GROUPS))
+        quantize_x(0)
+        opened = [open_tile(i) for i in range(OPEN_TILES)]
+        quantize_x(1)
 
-        def add_and_store(i, banks):
+        ends = list(accumulate(OUT_GROUPS))
+        for i in range(TILES):
+            banks = opened[i] if i < OPEN_TILES else open_tile(i)
+            multiply(1, i, banks)
             for h in range(HALVES):
                 b = i * HALVES + h
-                nc.vector.tensor_add(out=out_sb[:, b, :], in0=banks[h][:], in1=r_sb[:, b, :])
+                if b in SECOND_ADDER:
+                    nc.scalar.copy(out=out_sb[:, b, :], in_=banks[h][:])
+                    nc.gpsimd.tensor_add(out=out_sb[:, b, :], in0=out_sb[:, b, :], in1=r_sb[:, b, :])
+                else:
+                    nc.vector.tensor_add(out=out_sb[:, b, :], in0=banks[h][:], in1=r_sb[:, b, :])
                 if b + 1 in ends:
                     first = b + 1 - OUT_GROUPS[ends.index(b + 1)]
                     nc.sync.dma_start(out=out_banks[:, first : b + 1, :], in_=out_sb[:, first : b + 1, :])
-
-        def close_tiles(first, opened):
-            for i, banks in enumerate(opened, first):
-                multiply(1, i, banks)
-                add_and_store(i, banks)
-
-        interleave(nc.scalar.copy, 0, 0, slice(0, P))
-        quantize(0, 0)
-        interleave(nc.vector.tensor_copy, 0, 1, slice(0, 64))
-        interleave(nc.scalar.copy, 0, 1, slice(64, P))
-        quantize(0, 1)
-        opened = [open_tile(i) for i in range(OPEN_TILES)]
-
-        interleave(nc.vector.tensor_copy, 1, 0, slice(0, 76))
-        interleave(nc.scalar.copy, 1, 0, slice(76, P))
-        interleave(nc.vector.tensor_copy, 1, 1, slice(0, 32))
-        interleave(nc.scalar.copy, 1, 1, slice(32, P))
-        quantize(1, 0)
-        close_tiles(0, opened)
-        quantize(1, 1)
-
-        banks = open_tile(OPEN_TILES)
-        multiply(1, OPEN_TILES, banks)
-        opened = [open_tile(RUN + i) for i in range(OPEN_TILES)]
-        add_and_store(OPEN_TILES, banks)
-        close_tiles(RUN, opened)
-        close_tiles(TILES - 1, [open_tile(TILES - 1)])

@@ -19,16 +19,14 @@ PACK = 4
 K_PASS = P * PACK
 PASSES = K // K_PASS
 N_TILE = 512
-HALVES = N // N_TILE
-TILES = T // P
-BANKS = TILES * HALVES
-RUN = 4
 PLANE_START = (4, 0)
 OPEN_TILES = 4
 DMA_ALIGN = 4096
-R_GROUPS = (5, 4, 7)
-OUT_GROUPS = (9, 7)
-SECOND_ADDER = (0, 3, 5, 9, 11)
+TILES = T // P
+BANKS = TILES * (N // N_TILE)
+GROUPS = (2, 3, 3)
+VECTOR_COLS = 84
+SECOND_ADDER = (4, 10)
 
 
 def tile_mix_outl_tm_res_kernel(tc, x, w8_words, w8_scales, w4_words, w4_scales, r, out):
@@ -39,65 +37,72 @@ def tile_mix_outl_tm_res_kernel(tc, x, w8_words, w8_scales, w4_words, w4_scales,
         psum = ctx.enter_context(tc.psum_pool(name="psum", bufs=8))
         ctx.enter_context(tc.manual_schedule())
 
+        w_scales = [keep.tile([P, N], U8, align_bytes=DMA_ALIGN, name="w_scales%d" % g) for g in range(PASSES)]
         w8 = keep.tile([P, N], U32, align_bytes=DMA_ALIGN)
         w4 = keep.tile([P, 2 * N], U8, align_bytes=DMA_ALIGN)
-        w_scales = [keep.tile([P, N], U8, align_bytes=DMA_ALIGN, name="w_scales%d" % g) for g in range(PASSES)]
         x_raw = [keep.tile([P, PACK, T], F32, align_bytes=DMA_ALIGN, name="x_raw%d" % g) for g in range(PASSES)]
         x_codes = [keep.tile([P, T], U32, align_bytes=64, name="x_codes%d" % g) for g in range(PASSES)]
         x_scales = [keep.tile([P, T], U8, align_bytes=64, name="x_scales%d" % g) for g in range(PASSES)]
         r_sb = keep.tile([P, BANKS, N_TILE], F32, align_bytes=DMA_ALIGN)
         out_sb = keep.tile([P, BANKS, N_TILE], F32, align_bytes=DMA_ALIGN)
-        r_banks = r.rearrange("(p i) (h n) -> p (i h) n", i=TILES, n=N_TILE)
-        out_banks = out.rearrange("(p i) (h n) -> p (i h) n", i=TILES, n=N_TILE)
+        spans = [(end - count, end) for count, end in zip(GROUPS, accumulate(GROUPS))]
+
+        def in_hbm(matrix, first, end):
+            return matrix[first * P : end * P, :].rearrange("(p i) (h n) -> p (i h) n", p=P, n=N_TILE)
+
+        def in_sbuf(banks, first, end):
+            return banks[:, first * (N // N_TILE) : end * (N // N_TILE), :]
 
         def load_x(g):
             rows = x[g * K_PASS : (g + 1) * K_PASS, :]
             nc.sync.dma_start(out=x_raw[g][:], in_=rows.rearrange("(p j) t -> p j t", j=PACK))
 
-        def load_scales(queue, g, j, **how):
+        def load_scales(queue, g, which, **how):
             rows = (w8_scales, w4_scales)[g][0].rearrange("(q j) n -> j q n", j=4)
-            queue.dma_start(out=w_scales[g][PLANE_START[g] + j : P : 32, :].bitcast(I32), in_=rows[j].bitcast(I32), **how)
+            for j in which:
+                queue.dma_start(out=w_scales[g][PLANE_START[g] + j : P : 32, :].bitcast(I32), in_=rows[j].bitcast(I32), **how)
 
-        load_scales(nc.gpsimd, 1, 0, max_dma_last_dim=N // 2)
+        load_scales(nc.gpsimd, 1, range(2), max_dma_last_dim=N // 2)
         load_x(0)
         nc.scalar.dma_start(out=w8[:].bitcast(I32), in_=w8_words[0].rearrange("p n j -> p (n j)").bitcast(I32))
-        for j in range(4):
-            load_scales(nc.sync, 0, j)
-        load_scales(nc.sync, 1, 1)
+        load_scales(nc.sync, 0, range(4))
+        load_scales(nc.sync, 1, [2])
         load_x(1)
-        load_scales(nc.sync, 1, 2)
+        load_scales(nc.sync, 1, [3])
         nc.sync.dma_start(out=w4[:].bitcast(I32), in_=w4_words[0].bitcast(I32))
-        load_scales(nc.sync, 1, 3)
-        for count, end in zip(R_GROUPS, accumulate(R_GROUPS)):
-            nc.sync.dma_start(out=r_sb[:, end - count : end, :], in_=r_banks[:, end - count : end, :])
+        for first, end in spans:
+            nc.sync.dma_start(out=in_sbuf(r_sb, first, end), in_=in_hbm(r, first, end))
 
         def quantize_x(g):
-            by_tile = x_raw[g][:].rearrange("p j (m i) -> p m i j", i=TILES)
-            grouped = [keep.tile([P, RUN, P, PACK], BF16, align_bytes=64, name="grouped%d_%d" % (g, c)) for c in range(2)]
+            grouped = [
+                keep.tile([P, count, P, PACK], BF16, align_bytes=64, name="grouped%d_%d" % (g, c))
+                for c, count in enumerate(GROUPS)
+            ]
 
-            def interleave(copy, c, cols):
+            def interleave(c):
+                first, end = spans[c]
+                source = x_raw[g][:, :, first * P : end * P].rearrange("p j (m i) -> p m i j", m=P)
                 target = grouped[c][:].rearrange("p i m j -> p m i j")
-                copy(out=target[:, cols], in_=by_tile[:, cols, c * RUN : (c + 1) * RUN, :])
+                nc.vector.tensor_copy(out=target[:, :VECTOR_COLS], in_=source[:, :VECTOR_COLS])
+                nc.scalar.copy(out=target[:, VECTOR_COLS:], in_=source[:, VECTOR_COLS:])
 
             def quantize(c):
-                cols = slice(c * RUN * P, (c + 1) * RUN * P)
+                cols = slice(spans[c][0] * P, spans[c][1] * P)
                 nc.vector.quantize_mx(
                     out=x_codes[g][:, cols].bitcast(FP8X4),
                     scales=x_scales[g][:, cols],
                     in_=grouped[c][:].rearrange("p i m j -> p (i m j)"),
                 )
 
-            interleave(nc.vector.tensor_copy, 0, slice(0, 84))
-            interleave(nc.scalar.copy, 0, slice(84, P))
-            interleave(nc.scalar.copy, 1, slice(72, P))
-            interleave(nc.vector.tensor_copy, 1, slice(0, 32))
-            quantize(0)
-            interleave(nc.vector.tensor_copy, 1, slice(32, 72))
-            quantize(1)
+            interleave(0)
+            for c in range(1, len(GROUPS)):
+                interleave(c)
+                quantize(c - 1)
+            quantize(len(GROUPS) - 1)
 
         def multiply(g, i, banks):
             rows = slice(i * P, (i + 1) * P)
-            for h in range(HALVES):
+            for h in range(N // N_TILE):
                 cols = slice(h * N_TILE, (h + 1) * N_TILE)
                 if g == 0:
                     moving = w8[:, cols].bitcast(FP8X4)
@@ -114,7 +119,7 @@ def tile_mix_outl_tm_res_kernel(tc, x, w8_words, w8_scales, w4_words, w4_scales,
                 )
 
         def open_tile(i):
-            banks = [psum.tile([P, N_TILE], F32, name="bank") for h in range(HALVES)]
+            banks = [psum.tile([P, N_TILE], F32, name="bank") for h in range(N // N_TILE)]
             multiply(0, i, banks)
             return banks
 
@@ -122,17 +127,15 @@ def tile_mix_outl_tm_res_kernel(tc, x, w8_words, w8_scales, w4_words, w4_scales,
         opened = [open_tile(i) for i in range(OPEN_TILES)]
         quantize_x(1)
 
-        ends = list(accumulate(OUT_GROUPS))
-        for i in range(TILES):
-            banks = opened[i] if i < OPEN_TILES else open_tile(i)
-            multiply(1, i, banks)
-            for h in range(HALVES):
-                b = i * HALVES + h
-                if b in SECOND_ADDER:
-                    nc.scalar.copy(out=out_sb[:, b, :], in_=banks[h][:])
-                    nc.gpsimd.tensor_add(out=out_sb[:, b, :], in0=out_sb[:, b, :], in1=r_sb[:, b, :])
-                else:
-                    nc.vector.tensor_add(out=out_sb[:, b, :], in0=banks[h][:], in1=r_sb[:, b, :])
-                if b + 1 in ends:
-                    first = b + 1 - OUT_GROUPS[ends.index(b + 1)]
-                    nc.sync.dma_start(out=out_banks[:, first : b + 1, :], in_=out_sb[:, first : b + 1, :])
+        for first, end in spans:
+            for i in range(first, end):
+                banks = opened[i] if i < OPEN_TILES else open_tile(i)
+                multiply(1, i, banks)
+                for h in range(N // N_TILE):
+                    b = i * (N // N_TILE) + h
+                    if b in SECOND_ADDER:
+                        nc.scalar.copy(out=out_sb[:, b, :], in_=banks[h][:])
+                        nc.gpsimd.tensor_add(out=out_sb[:, b, :], in0=out_sb[:, b, :], in1=r_sb[:, b, :])
+                    else:
+                        nc.vector.tensor_add(out=out_sb[:, b, :], in0=banks[h][:], in1=r_sb[:, b, :])
+            nc.sync.dma_start(out=in_hbm(out, first, end), in_=in_sbuf(out_sb, first, end))

@@ -19,14 +19,14 @@ PACK = 4
 K_PASS = P * PACK
 PASSES = K // K_PASS
 N_TILE = 512
-PLANE_START = (4, 0)
-OPEN_TILES = 4
-DMA_ALIGN = 4096
+HALVES = N // N_TILE
 TILES = T // P
-BANKS = TILES * (N // N_TILE)
-GROUPS = (2, 3, 3)
-VECTOR_COLS = 84
-SECOND_ADDER = (4, 10)
+BANKS = TILES * HALVES
+RUN = 4
+PLANE_START = (4, 0)
+DMA_ALIGN = 4096
+R_GROUPS = (5, 5, 6)
+OUT_GROUPS = (6, 5, 5)
 
 
 def tile_mix_outl_tm_res_kernel(tc, x, w8_words, w8_scales, w4_words, w4_scales, r, out):
@@ -37,72 +37,60 @@ def tile_mix_outl_tm_res_kernel(tc, x, w8_words, w8_scales, w4_words, w4_scales,
         psum = ctx.enter_context(tc.psum_pool(name="psum", bufs=8))
         ctx.enter_context(tc.manual_schedule())
 
-        w_scales = [keep.tile([P, N], U8, align_bytes=DMA_ALIGN, name="w_scales%d" % g) for g in range(PASSES)]
         w8 = keep.tile([P, N], U32, align_bytes=DMA_ALIGN)
         w4 = keep.tile([P, 2 * N], U8, align_bytes=DMA_ALIGN)
+        w_scales = [keep.tile([P, N], U8, align_bytes=DMA_ALIGN, name="w_scales%d" % g) for g in range(PASSES)]
         x_raw = [keep.tile([P, PACK, T], F32, align_bytes=DMA_ALIGN, name="x_raw%d" % g) for g in range(PASSES)]
         x_codes = [keep.tile([P, T], U32, align_bytes=64, name="x_codes%d" % g) for g in range(PASSES)]
         x_scales = [keep.tile([P, T], U8, align_bytes=64, name="x_scales%d" % g) for g in range(PASSES)]
         r_sb = keep.tile([P, BANKS, N_TILE], F32, align_bytes=DMA_ALIGN)
         out_sb = keep.tile([P, BANKS, N_TILE], F32, align_bytes=DMA_ALIGN)
-        spans = [(end - count, end) for count, end in zip(GROUPS, accumulate(GROUPS))]
-
-        def in_hbm(matrix, first, end):
-            return matrix[first * P : end * P, :].rearrange("(p i) (h n) -> p (i h) n", p=P, n=N_TILE)
-
-        def in_sbuf(banks, first, end):
-            return banks[:, first * (N // N_TILE) : end * (N // N_TILE), :]
+        r_banks = r.rearrange("(p i) (h n) -> p (i h) n", i=TILES, n=N_TILE)
+        out_banks = out.rearrange("(p i) (h n) -> p (i h) n", i=TILES, n=N_TILE)
 
         def load_x(g):
             rows = x[g * K_PASS : (g + 1) * K_PASS, :]
             nc.sync.dma_start(out=x_raw[g][:], in_=rows.rearrange("(p j) t -> p j t", j=PACK))
 
-        def load_scales(queue, g, which, **how):
+        def load_scales(queue, g, j, **how):
             rows = (w8_scales, w4_scales)[g][0].rearrange("(q j) n -> j q n", j=4)
-            for j in which:
-                queue.dma_start(out=w_scales[g][PLANE_START[g] + j : P : 32, :].bitcast(I32), in_=rows[j].bitcast(I32), **how)
+            queue.dma_start(out=w_scales[g][PLANE_START[g] + j : P : 32, :].bitcast(I32), in_=rows[j].bitcast(I32), **how)
 
-        load_scales(nc.gpsimd, 1, range(2), max_dma_last_dim=N // 2)
+        for j in range(2):
+            load_scales(nc.gpsimd, 0, j, max_dma_last_dim=N // 2)
         load_x(0)
         nc.scalar.dma_start(out=w8[:].bitcast(I32), in_=w8_words[0].rearrange("p n j -> p (n j)").bitcast(I32))
-        load_scales(nc.sync, 0, range(4))
-        load_scales(nc.sync, 1, [2])
+        for j in range(2):
+            load_scales(nc.sync, 0, 2 + j)
+            load_scales(nc.sync, 1, j)
         load_x(1)
-        load_scales(nc.sync, 1, [3])
+        load_scales(nc.sync, 1, 2)
         nc.sync.dma_start(out=w4[:].bitcast(I32), in_=w4_words[0].bitcast(I32))
-        for first, end in spans:
-            nc.sync.dma_start(out=in_sbuf(r_sb, first, end), in_=in_hbm(r, first, end))
+        load_scales(nc.sync, 1, 3)
+        for count, end in zip(R_GROUPS, accumulate(R_GROUPS)):
+            nc.sync.dma_start(out=r_sb[:, end - count : end, :], in_=r_banks[:, end - count : end, :])
 
-        def quantize_x(g):
-            grouped = [
-                keep.tile([P, count, P, PACK], BF16, align_bytes=64, name="grouped%d_%d" % (g, c))
-                for c, count in enumerate(GROUPS)
-            ]
+        grouped = [
+            [keep.tile([P, RUN, P, PACK], BF16, align_bytes=64, name="grouped%d_%d" % (g, c)) for c in range(TILES // RUN)]
+            for g in range(PASSES)
+        ]
 
-            def interleave(c):
-                first, end = spans[c]
-                source = x_raw[g][:, :, first * P : end * P].rearrange("p j (m i) -> p m i j", m=P)
-                target = grouped[c][:].rearrange("p i m j -> p m i j")
-                nc.vector.tensor_copy(out=target[:, :VECTOR_COLS], in_=source[:, :VECTOR_COLS])
-                nc.scalar.copy(out=target[:, VECTOR_COLS:], in_=source[:, VECTOR_COLS:])
+        def interleave(copy, g, c, cols):
+            by_tile = x_raw[g][:].rearrange("p j (m i) -> p m i j", i=TILES)
+            target = grouped[g][c][:].rearrange("p i m j -> p m i j")
+            copy(out=target[:, cols], in_=by_tile[:, cols, c * RUN : (c + 1) * RUN, :])
 
-            def quantize(c):
-                cols = slice(spans[c][0] * P, spans[c][1] * P)
-                nc.vector.quantize_mx(
-                    out=x_codes[g][:, cols].bitcast(FP8X4),
-                    scales=x_scales[g][:, cols],
-                    in_=grouped[c][:].rearrange("p i m j -> p (i m j)"),
-                )
-
-            interleave(0)
-            for c in range(1, len(GROUPS)):
-                interleave(c)
-                quantize(c - 1)
-            quantize(len(GROUPS) - 1)
+        def quantize(g, c):
+            cols = slice(c * RUN * P, (c + 1) * RUN * P)
+            nc.vector.quantize_mx(
+                out=x_codes[g][:, cols].bitcast(FP8X4),
+                scales=x_scales[g][:, cols],
+                in_=grouped[g][c][:].rearrange("p i m j -> p (i m j)"),
+            )
 
         def multiply(g, i, banks):
             rows = slice(i * P, (i + 1) * P)
-            for h in range(N // N_TILE):
+            for h in range(HALVES):
                 cols = slice(h * N_TILE, (h + 1) * N_TILE)
                 if g == 0:
                     moving = w8[:, cols].bitcast(FP8X4)
@@ -119,23 +107,41 @@ def tile_mix_outl_tm_res_kernel(tc, x, w8_words, w8_scales, w4_words, w4_scales,
                 )
 
         def open_tile(i):
-            banks = [psum.tile([P, N_TILE], F32, name="bank") for h in range(N // N_TILE)]
+            banks = [psum.tile([P, N_TILE], F32, name="bank") for h in range(HALVES)]
             multiply(0, i, banks)
             return banks
 
-        quantize_x(0)
-        opened = [open_tile(i) for i in range(OPEN_TILES)]
-        quantize_x(1)
+        ends = list(accumulate(OUT_GROUPS))
 
-        for first, end in spans:
-            for i in range(first, end):
-                banks = opened[i] if i < OPEN_TILES else open_tile(i)
-                multiply(1, i, banks)
-                for h in range(N // N_TILE):
-                    b = i * (N // N_TILE) + h
-                    if b in SECOND_ADDER:
-                        nc.scalar.copy(out=out_sb[:, b, :], in_=banks[h][:])
-                        nc.gpsimd.tensor_add(out=out_sb[:, b, :], in0=out_sb[:, b, :], in1=r_sb[:, b, :])
-                    else:
-                        nc.vector.tensor_add(out=out_sb[:, b, :], in0=banks[h][:], in1=r_sb[:, b, :])
-            nc.sync.dma_start(out=in_hbm(out, first, end), in_=in_sbuf(out_sb, first, end))
+        def add_and_store(i, banks):
+            for h in range(HALVES):
+                b = i * HALVES + h
+                nc.vector.tensor_add(out=out_sb[:, b, :], in0=banks[h][:], in1=r_sb[:, b, :])
+                if b + 1 in ends:
+                    first = b + 1 - OUT_GROUPS[ends.index(b + 1)]
+                    nc.sync.dma_start(out=out_banks[:, first : b + 1, :], in_=out_sb[:, first : b + 1, :])
+
+        def share_copies(g, first_split, second_split):
+            for c, split in enumerate((first_split, second_split)):
+                interleave(nc.vector.tensor_copy, g, c, slice(0, split))
+                interleave(nc.scalar.copy, g, c, slice(split, P))
+
+        share_copies(0, 84, 84)
+        quantize(0, 0)
+        quantize(0, 1)
+        banks = [open_tile(i) for i in range(RUN)]
+
+        share_copies(1, 84, 24)
+        quantize(1, 0)
+        for i in range(RUN):
+            multiply(1, i, banks[i])
+        for i in range(RUN - 1):
+            add_and_store(i, banks[i])
+            banks.append(open_tile(RUN + i))
+        quantize(1, 1)
+        add_and_store(RUN - 1, banks[RUN - 1])
+        for i in range(RUN, TILES):
+            if i == TILES - 1:
+                banks.append(open_tile(i))
+            multiply(1, i, banks[i])
+            add_and_store(i, banks[i])

from contextlib import ExitStack
from itertools import accumulate

import concourse.mybir as mybir

K, T, N = 1024, 1024, 1024
FLOPS = 2 * K * T * N

F32 = mybir.dt.float32
BF16 = mybir.dt.bfloat16
I32 = mybir.dt.int32
U32 = mybir.dt.uint32
U8 = mybir.dt.uint8
FP8X4 = mybir.dt.float8_e4m3fn_x4
FP4X4 = mybir.dt.float4_e2m1fn_x4

P = 128
PACK = 4
K_PASS = P * PACK
PASSES = K // K_PASS
N_TILE = 512
HALVES = N // N_TILE
TILES = T // P
BANKS = TILES * HALVES
RUN = 4
PLANE_START = (4, 0)
DMA_ALIGN = 4096
R_GROUPS = (5, 5, 6)
OUT_GROUPS = (6, 5, 5)


def tile_mix_outl_tm_res_kernel(tc, x, w8_words, w8_scales, w4_words, w4_scales, r, out):
    nc = tc.nc

    with ExitStack() as ctx:
        keep = ctx.enter_context(tc.tile_pool(name="keep", bufs=1))
        psum = ctx.enter_context(tc.psum_pool(name="psum", bufs=8))
        ctx.enter_context(tc.manual_schedule())

        w8 = keep.tile([P, N], U32, align_bytes=DMA_ALIGN)
        w4 = keep.tile([P, 2 * N], U8, align_bytes=DMA_ALIGN)
        w_scales = [keep.tile([P, N], U8, align_bytes=DMA_ALIGN, name="w_scales%d" % g) for g in range(PASSES)]
        x_raw = [keep.tile([P, PACK, T], F32, align_bytes=DMA_ALIGN, name="x_raw%d" % g) for g in range(PASSES)]
        x_codes = [keep.tile([P, T], U32, align_bytes=64, name="x_codes%d" % g) for g in range(PASSES)]
        x_scales = [keep.tile([P, T], U8, align_bytes=64, name="x_scales%d" % g) for g in range(PASSES)]
        r_sb = keep.tile([P, BANKS, N_TILE], F32, align_bytes=DMA_ALIGN)
        out_sb = keep.tile([P, BANKS, N_TILE], F32, align_bytes=DMA_ALIGN)
        r_banks = r.rearrange("(p i) (h n) -> p (i h) n", i=TILES, n=N_TILE)
        out_banks = out.rearrange("(p i) (h n) -> p (i h) n", i=TILES, n=N_TILE)

        def load_x(g):
            rows = x[g * K_PASS : (g + 1) * K_PASS, :]
            nc.sync.dma_start(out=x_raw[g][:], in_=rows.rearrange("(p j) t -> p j t", j=PACK))

        def load_scales(queue, g, j, **how):
            rows = (w8_scales, w4_scales)[g][0].rearrange("(q j) n -> j q n", j=4)
            queue.dma_start(out=w_scales[g][PLANE_START[g] + j : P : 32, :].bitcast(I32), in_=rows[j].bitcast(I32), **how)

        for j in range(2):
            load_scales(nc.gpsimd, 0, j, max_dma_last_dim=N // 2)
        load_x(0)
        nc.scalar.dma_start(out=w8[:].bitcast(I32), in_=w8_words[0].rearrange("p n j -> p (n j)").bitcast(I32))
        for j in range(2):
            load_scales(nc.sync, 0, 2 + j)
            load_scales(nc.sync, 1, j)
        load_x(1)
        load_scales(nc.sync, 1, 2)
        nc.sync.dma_start(out=w4[:].bitcast(I32), in_=w4_words[0].bitcast(I32))
        load_scales(nc.sync, 1, 3)
        for count, end in zip(R_GROUPS, accumulate(R_GROUPS)):
            nc.sync.dma_start(out=r_sb[:, end - count : end, :], in_=r_banks[:, end - count : end, :])

        grouped = [
            [keep.tile([P, RUN, P, PACK], BF16, align_bytes=64, name="grouped%d_%d" % (g, c)) for c in range(TILES // RUN)]
            for g in range(PASSES)
        ]

        def interleave(copy, g, c, cols):
            by_tile = x_raw[g][:].rearrange("p j (m i) -> p m i j", i=TILES)
            target = grouped[g][c][:].rearrange("p i m j -> p m i j")
            copy(out=target[:, cols], in_=by_tile[:, cols, c * RUN : (c + 1) * RUN, :])

        def quantize(g, c):
            cols = slice(c * RUN * P, (c + 1) * RUN * P)
            nc.vector.quantize_mx(
                out=x_codes[g][:, cols].bitcast(FP8X4),
                scales=x_scales[g][:, cols],
                in_=grouped[g][c][:].rearrange("p i m j -> p (i m j)"),
            )

        def multiply(g, i, banks):
            rows = slice(i * P, (i + 1) * P)
            for h in range(HALVES):
                cols = slice(h * N_TILE, (h + 1) * N_TILE)
                if g == 0:
                    moving = w8[:, cols].bitcast(FP8X4)
                else:
                    moving = w4[:, 2 * cols.start : 2 * cols.stop].bitcast(FP4X4)
                nc.tensor.matmul_mx(
                    out=banks[h][:],
                    lhsT=x_codes[g][:, rows].bitcast(FP8X4),
                    lhsT_scale=x_scales[g][:, rows],
                    rhs=moving,
                    rhs_scale=w_scales[g][PLANE_START[g] :, cols],
                    start=(g == 0),
                    stop=(g == PASSES - 1),
                )

        def open_tile(i):
            banks = [psum.tile([P, N_TILE], F32, name="bank") for h in range(HALVES)]
            multiply(0, i, banks)
            return banks

        ends = list(accumulate(OUT_GROUPS))

        def add_and_store(i, banks):
            for h in range(HALVES):
                b = i * HALVES + h
                nc.vector.tensor_add(out=out_sb[:, b, :], in0=banks[h][:], in1=r_sb[:, b, :])
                if b + 1 in ends:
                    first = b + 1 - OUT_GROUPS[ends.index(b + 1)]
                    nc.sync.dma_start(out=out_banks[:, first : b + 1, :], in_=out_sb[:, first : b + 1, :])

        def share_copies(g, first_split, second_split):
            for c, split in enumerate((first_split, second_split)):
                interleave(nc.vector.tensor_copy, g, c, slice(0, split))
                interleave(nc.scalar.copy, g, c, slice(split, P))

        share_copies(0, 84, 84)
        quantize(0, 0)
        quantize(0, 1)
        banks = [open_tile(i) for i in range(RUN)]

        share_copies(1, 84, 24)
        quantize(1, 0)
        for i in range(RUN):
            multiply(1, i, banks[i])
        for i in range(RUN - 1):
            add_and_store(i, banks[i])
            banks.append(open_tile(RUN + i))
        quantize(1, 1)
        add_and_store(RUN - 1, banks[RUN - 1])
        for i in range(RUN, TILES):
            if i == TILES - 1:
                banks.append(open_tile(i))
            multiply(1, i, banks[i])
            add_and_store(i, banks[i])
